import numpy as np
import ml_dtypes


def mxq(x, axis, fmt="e4m3"):
    dtype, down = {"e4m3": (ml_dtypes.float8_e4m3fn, 7), "e5m2": (ml_dtypes.float8_e5m2, 14)}[fmt]
    v = np.moveaxis(np.asarray(x, np.float32).astype(ml_dtypes.bfloat16).astype(np.float64), axis, -1)
    blocks = v.reshape(v.shape[:-1] + (-1, 32))
    amax = np.abs(blocks).max(-1, keepdims=True)
    byte = np.maximum(np.where(amax > 0, np.frexp(amax)[1] - 1 + 127, 0) - down, 1)
    scale = np.exp2(byte - 127.0)
    codes = (blocks / scale).astype(np.float32).astype(dtype).astype(np.float64)
    return np.moveaxis((codes * scale).reshape(v.shape), -1, axis)


WIDE = False


def mx_kscale(k):
    if not WIDE:
        return np.ones(k)
    levels = np.array([10, -10, 5, -5, 0])
    if k % 512:
        return np.exp2(np.random.permutation(np.resize(levels, k // 32))).repeat(32)
    a = np.empty((k // 512, 16))
    for p in range(k // 512):
        a[p, :8] = np.random.permutation(np.resize(levels, 8))
        for g in range(8):
            far = levels[np.abs(levels - a[p, g]) >= 10]
            a[p, g + 8] = far[np.random.randint(len(far))]
    return np.exp2(a.ravel()).repeat(32)


def f64(x):
    return np.asarray(x).astype(np.float64)


def striped(idx):
    return np.tile(np.asarray(idx).reshape(-1, 16).T, (8, 1)).astype(np.uint16)


def unstriped(offs):
    return offs[:16].T.reshape(-1).astype(np.int64)


E2M1 = np.array([0.0, 0.5, 1.0, 1.5, 2.0, 3.0, 4.0, 6.0, -0.0, -0.5, -1.0, -1.5, -2.0, -3.0, -4.0, -6.0])


def pack_weight(w, fmt):
    k, n = w.shape
    w = f64(np.asarray(w, np.float32).astype(ml_dtypes.bfloat16)).reshape(k // 32, 32, n)
    amax = np.abs(w).max(1)
    if fmt == "e4m3":
        byte = np.frexp(amax)[1] - 1 + 127 - 7
    else:
        mant, ex = np.frexp(amax / 6.0)
        byte = np.where(mant > 0.5, ex, ex - 1) + 127
    byte = np.clip(np.where(amax > 0, byte, 1), 1, 254)
    scaled = (w * np.exp2(127.0 - byte)[:, None, :]).reshape(k, n).astype(np.float32)
    by_word = np.ascontiguousarray(scaled.reshape(k // 512, 128, 4, n).transpose(0, 1, 3, 2))
    if fmt == "e4m3":
        words = by_word.astype(ml_dtypes.float8_e4m3fn).view(np.uint8)
    else:
        c = by_word.astype(ml_dtypes.float4_e2m1fn).view(np.uint8) & 0xF
        words = (c[..., 0::2] | (c[..., 1::2] << 4)).reshape(k // 512, 128, 2 * n)
    return np.ascontiguousarray(words), np.ascontiguousarray(byte.astype(np.uint8).reshape(k // 512, 16, n))


def unpack_weight(words, scales, fmt):
    g, _, n = scales.shape
    words = np.ascontiguousarray(words).reshape(g, 128, n, -1)
    if fmt == "e4m3":
        vals = words.view(ml_dtypes.float8_e4m3fn).astype(np.float64)
    else:
        nib = np.empty((g, 128, n, 4), np.uint8)
        nib[..., 0::2] = words & 0xF
        nib[..., 1::2] = words >> 4
        vals = E2M1[nib]
    vals = vals * np.repeat(np.exp2(scales.astype(np.float64) - 127.0), 8, axis=1)[..., None]
    return vals.transpose(0, 1, 3, 2).reshape(g * 512, n)


K, I, L, S, T, N = 1024, 512, 512, 512, 512, 512


def setup_inputs():
    n = np.random.standard_normal
    idx = np.random.randint(0, I, T)
    idx2 = np.random.randint(0, S, T)
    fk = mx_kscale(K)
    fl = mx_kscale(L)
    xap = pack_weight(n((K, I)) / fk[:, None], "e4m3")
    xbp = pack_weight(n((L, S)) / fl[:, None], "e2m1")
    wbp = pack_weight(n((L, N)) * np.random.uniform(0.2, 2.0, (1, N)) / np.sqrt(L) * fl[:, None], "e4m3")
    return {
        "xa_words": xap[0],
        "xa_scales": xap[1],
        "wa": (n((K, N)) * np.random.uniform(0.2, 2.0, (1, N)) / np.sqrt(K) * fk[:, None]).astype(np.float32),
        "xb_words": xbp[0],
        "xb_scales": xbp[1],
        "wb_words": wbp[0],
        "wb_scales": wbp[1],
        "ga": (np.random.uniform(0.3, 1.0, (1, T))).astype(np.float32),
        "gb": (np.random.uniform(0.3, 1.0, (1, T))).astype(np.float32),
        "offs": striped(idx),
        "offs2": striped(idx2),
    }


def reference(xa_words, xa_scales, wa, xb_words, xb_scales, wb_words, wb_scales, ga, gb, offs, offs2):
    idx = unstriped(offs)
    idx2 = unstriped(offs2)
    xau = unpack_weight(xa_words, xa_scales, "e4m3")
    xbu = unpack_weight(xb_words, xb_scales, "e2m1")
    wbu = unpack_weight(wb_words, wb_scales, "e4m3")
    waq = mxq(f64(wa), 0, "e4m3")
    za = waq.T @ xau
    zb = wbu.T @ xbu
    ra = 1.0 / np.sqrt(np.mean(np.square(za), axis=1, keepdims=True) + 0.01)
    rb = 1.0 / np.sqrt(np.mean(np.square(zb), axis=1, keepdims=True) + 0.01)
    y = f64(ga) * ra * za[:, idx] + f64(gb) * rb * zb[:, idx2]
    return y

from contextlib import ExitStack

import concourse.mybir as mybir
from concourse.masks import make_identity

K, L, SLOTS, T, N = 1024, 512, 512, 512, 512
FLOPS = 2 * N * SLOTS * (K + L)

F32 = mybir.dt.float32
BF16 = mybir.dt.bfloat16
I32 = mybir.dt.int32
U32 = mybir.dt.uint32
U16 = mybir.dt.uint16
U8 = mybir.dt.uint8
FP8X4 = mybir.dt.float8_e4m3fn_x4
FP4X4 = mybir.dt.float4_e2m1fn_x4
ACT = mybir.ActivationFunctionType
ALU = mybir.AluOpType

P = 128
PACK = 4
K_PASS = P * PACK
PASSES = K // K_PASS
BLOCKS = N // P
HALF = N // 2
PAD = 8
EPS = 0.01


def tile_moe_combine_evened_buffers_kernel(
    tc, xa_words, xa_scales, wa, xb_words, xb_scales, wb_words, wb_scales, ga, gb, offs, offs2, out
):
    nc = tc.nc
    with ExitStack() as ctx:
        keep = ctx.enter_context(tc.tile_pool(name="keep", bufs=1))
        ring = ctx.enter_context(tc.tile_pool(name="ring", bufs=2))
        psum = ctx.enter_context(tc.psum_pool(name="psum", bufs=1))

        list_a = keep.tile([P, T // 16], U16, name="list_a")
        list_b = keep.tile([P, T // 16], U16, name="list_b")
        wb_codes = keep.tile([P, N], U32, name="wb_codes", align_bytes=64)
        wb_plane = keep.tile([P, N], U8, name="wb_plane", align_bytes=64)
        xb_codes = keep.tile([P, 2 * SLOTS], U8, name="xb_codes", align_bytes=64)
        xb_plane = keep.tile([P, SLOTS], U8, name="xb_plane", align_bytes=64)
        xa_codes = keep.tile([P, PASSES, SLOTS], U32, name="xa_codes", align_bytes=64)
        xa_plane = keep.tile([P, PASSES * SLOTS], U8, name="xa_plane", align_bytes=64)
        units = [(z, h) for h in range(2) for z in range(PASSES)]
        wa_raw = {u: keep.tile([P, PACK, HALF], F32, name=f"wa_raw{u[0]}{u[1]}") for u in units}
        wa_bf = {u: keep.tile([P, HALF, PACK], BF16, name=f"wa_bf{u[0]}{u[1]}", align_bytes=64) for u in units}
        wa_codes = {u: keep.tile([P, HALF], U32, name=f"wa_codes{u[0]}{u[1]}", align_bytes=64) for u in units}
        wa_plane = {u: keep.tile([P, HALF], U8, name=f"wa_plane{u[0]}{u[1]}", align_bytes=64) for u in units}
        ga_col = keep.tile([P, 2, 2], F32, name="ga_col")
        gb_col = keep.tile([P, 2, 2], F32, name="gb_col")
        ga_rows = keep.tile([P, T], F32, name="ga_rows")
        gb_rows = keep.tile([P, T], F32, name="gb_rows")
        ident = keep.tile([P, P], F32, name="ident")
        eps = keep.tile([P, 1], F32, name="eps")
        warm = keep.tile([P, 1], F32, name="warm")
        za = [keep.tile([P, SLOTS + PAD], F32, name=f"za{j}") for j in range(BLOCKS)]
        zb = [keep.tile([P, SLOTS + PAD], F32, name=f"zb{j}") for j in range(BLOCKS)]
        pa = [keep.tile([P, T], F32, name=f"pa{j}") for j in range(BLOCKS)]
        pb = [keep.tile([P, T], F32, name=f"pb{j}") for j in range(BLOCKS)]
        res = [keep.tile([P, T], F32, name=f"res{j}") for j in range(BLOCKS)]
        ssq = {(s, j): keep.tile([P, 1], F32, name=f"ssq_{s}{j}") for s in "ab" for j in range(BLOCKS)}
        rinv = {(s, j): keep.tile([P, 1], F32, name=f"rinv_{s}{j}") for s in "ab" for j in range(BLOCKS)}

        def load_plane_quadrant(queue, plane, scales, q):
            rows = scales[0, 4 * q : 4 * q + 4, :].bitcast(I32)
            queue.dma_start(out=plane[32 * q : 32 * q + 32, :].bitcast(I32), in_=rows.partition_broadcast(8))

        def load_gate(queue, col, gate):
            queue.dma_start(out=col[:], in_=gate.rearrange("o (h p e) -> p (o h) e", h=2, e=2))

        def load_wa(u):
            z, h = u
            rows = wa[z * K_PASS : (z + 1) * K_PASS, h * HALF : (h + 1) * HALF]
            nc.sync.dma_start(out=wa_raw[u][:], in_=rows.rearrange("(p t) n -> p t n", t=PACK))

        make_identity(nc, ident[:])
        nc.vector.memset(eps[:], 1.0)
        nc.vector.tensor_scalar_mul(eps[:], eps[:], EPS)
        nc.vector.memset(xa_plane[:].bitcast(I32), 0)
        for tile in zb + za:
            nc.vector.memset(tile[:, SLOTS:], 0.0)

        load_gate(nc.sync, gb_col, gb)
        load_gate(nc.gpsimd, ga_col, ga)
        load_plane_quadrant(nc.scalar, wb_plane, wb_scales, 0)
        load_plane_quadrant(nc.sync, wb_plane, wb_scales, 1)
        load_plane_quadrant(nc.scalar, wb_plane, wb_scales, 2)
        load_plane_quadrant(nc.sync, wb_plane, wb_scales, 3)
        nc.sync.dma_start(out=wb_codes[:].bitcast(I32), in_=wb_words[0].rearrange("p n t -> p (n t)").bitcast(I32))
        nc.sync.dma_start(out=xb_codes[:].bitcast(I32), in_=xb_words[0].bitcast(I32))
        load_wa(units[0])
        for q in range(4):
            load_plane_quadrant(nc.sync, xb_plane, xb_scales, q)
        load_wa(units[1])
        nc.sync.dma_start(list_b[:], offs2)
        nc.sync.dma_start(
            out=xa_codes[:].bitcast(I32), in_=xa_words.rearrange("z p n t -> p z (n t)").bitcast(I32)
        )
        for q in range(4):
            nc.sync.dma_start(
                out=xa_plane[32 * q : 32 * q + 4, :].bitcast(I32).rearrange("r (z c) -> r z c", z=PASSES),
                in_=xa_scales[:, 4 * q : 4 * q + 4, :].bitcast(I32).rearrange("z r c -> r z c"),
            )
        load_wa(units[2])
        load_wa(units[3])
        nc.sync.dma_start(list_a[:], offs)

        nc.scalar.activation(warm[:], eps[:], ACT.Abs_reciprocal_sqrt)

        def spread(col, rows, tags):
            for h, tag in enumerate(tags):
                halfbank = psum.tile([P, 2, P], F32, name=tag, tag=tag)
                for e in range(2):
                    nc.tensor.transpose(halfbank[:, e, :], col[:, h, e : e + 1].to_broadcast([P, P]), ident[:])
                nc.scalar.copy(
                    out=rows[:, h * HALF : (h + 1) * HALF].rearrange("p (n e) -> p n e", e=2),
                    in_=halfbank[:].rearrange("p e n -> p n e"),
                )

        spread(gb_col, gb_rows, ("bank_b0", "bank_b1"))
        spread(ga_col, ga_rows, ("bank_b2", "bank_b3"))

        def cast(copy, u):
            copy(
                out=wa_bf[u][:].rearrange("p (c i) t -> p c t i", i=4),
                in_=wa_raw[u][:].rearrange("p t (c i) -> p c t i", i=4),
            )

        def quantize(u):
            nc.vector.quantize_mx(
                out=wa_codes[u][:].bitcast(FP8X4),
                scales=wa_plane[u][:],
                in_=wa_bf[u][:].rearrange("p n t -> p (n t)"),
            )

        bank = {}

        def product_b(j):
            cols = slice(j * P, (j + 1) * P)
            bank["b", j] = psum.tile([P, SLOTS], F32, name=f"bank_b{j}", tag=f"bank_b{j}")
            nc.tensor.matmul_mx(
                out=bank["b", j][:],
                lhsT=wb_codes[:, cols].bitcast(FP8X4),
                lhsT_scale=wb_plane[:, cols],
                rhs=xb_codes[:].bitcast(FP4X4),
                rhs_scale=xb_plane[:],
                start=True,
                stop=True,
            )

        def product_a(j):
            h, cols = j // 2, slice((j % 2) * P, (j % 2 + 1) * P)
            bank["a", j] = psum.tile([P, SLOTS], F32, name=f"bank_a{j}", tag=f"bank_a{j}")
            for z in range(PASSES):
                nc.tensor.matmul_mx(
                    out=bank["a", j][:],
                    lhsT=wa_codes[z, h][:, cols].bitcast(FP8X4),
                    lhsT_scale=wa_plane[z, h][:, cols],
                    rhs=xa_codes[:, z, :].bitcast(FP8X4),
                    rhs_scale=xa_plane[:, z * SLOTS : (z + 1) * SLOTS],
                    start=(z == 0),
                    stop=(z == PASSES - 1),
                )

        def squares(s, j):
            junk = ring.tile([P, SLOTS], BF16, name="junk")
            nc.scalar.activation(junk[:], bank[s, j][:], ACT.Square, accum_out=ssq[s, j][:])

        def root(s, j):
            nc.scalar.activation(
                rinv[s, j][:], ssq[s, j][:], ACT.Abs_reciprocal_sqrt, bias=eps[:], scale=1.0 / SLOTS
            )

        def evict_b(j):
            nc.scalar.copy(zb[j][:, :SLOTS], bank["b", j][:])

        def evict_a(j):
            nc.scalar.activation(za[j][:, :SLOTS], bank["a", j][:], ACT.Copy, scale=rinv["a", j][:])

        def gather_b(j):
            nc.vector.tensor_tensor(pb[j][:], zb[j][:].indirect(list_b[:]), gb_rows[:], ALU.mult)

        def gather_a(j):
            nc.vector.tensor_tensor(pa[j][:], za[j][:].indirect(list_a[:]), ga_rows[:], ALU.mult)

        def finish(j):
            nc.vector.scalar_tensor_tensor(res[j][:], pb[j][:], rinv["b", j][:], pa[j][:], ALU.mult, ALU.add)
            nc.sync.dma_start(out=out[j * P : (j + 1) * P, :], in_=res[j][:])

        cast(nc.vector.tensor_copy, units[0])
        for j in range(BLOCKS):
            product_b(j)
        evict_b(0)
        quantize(units[0])
        cast(nc.vector.tensor_copy, units[1])
        evict_b(1)
        gather_b(0)
        quantize(units[1])
        evict_b(2)
        evict_b(3)
        product_a(0)
        product_a(1)
        gather_b(1)
        cast(nc.scalar.copy, units[2])
        gather_b(2)
        squares("a", 0)
        quantize(units[2])
        cast(nc.scalar.copy, units[3])
        root("a", 0)
        squares("a", 1)
        evict_a(0)
        gather_b(3)
        quantize(units[3])
        root("a", 1)
        evict_a(1)
        product_a(2)
        product_a(3)
        gather_a(0)
        squares("b", 0)
        squares("a", 2)
        root("b", 0)
        root("a", 2)
        evict_a(2)
        gather_a(1)
        finish(0)
        squares("a", 3)
        squares("b", 1)
        root("a", 3)
        evict_a(3)
        root("b", 1)
        gather_a(2)
        finish(1)
        squares("b", 2)
        squares("b", 3)
        root("b", 2)
        root("b", 3)
        gather_a(3)
        finish(2)
        finish(3)
